import numpy as np
import ml_dtypes


def mxq(x, axis, fmt="e4m3"):
    dtype, down = {"e4m3": (ml_dtypes.float8_e4m3fn, 7), "e5m2": (ml_dtypes.float8_e5m2, 14)}[fmt]
    v = np.moveaxis(np.asarray(x, np.float32).astype(ml_dtypes.bfloat16).astype(np.float64), axis, -1)
    blocks = v.reshape(v.shape[:-1] + (-1, 32))
    amax = np.abs(blocks).max(-1, keepdims=True)
    byte = np.maximum(np.where(amax > 0, np.frexp(amax)[1] - 1 + 127, 0) - down, 1)
    scale = np.exp2(byte - 127.0)
    codes = (blocks / scale).astype(np.float32).astype(dtype).astype(np.float64)
    return np.moveaxis((codes * scale).reshape(v.shape), -1, axis)


WIDE = False


def mx_kscale(k):
    if not WIDE:
        return np.ones(k)
    levels = np.array([30, -30])
    if k % 512:
        return np.exp2(np.random.permutation(np.resize(levels, k // 32))).repeat(32)
    a = np.empty((k // 512, 16))
    for p in range(k // 512):
        a[p, :8] = np.random.permutation(np.resize(levels, 8))
        for g in range(8):
            far = levels[np.abs(levels - a[p, g]) >= 10]
            a[p, g + 8] = far[np.random.randint(len(far))]
    return np.exp2(a.ravel()).repeat(32)


def f64(x):
    return np.asarray(x).astype(np.float64)


def striped(idx):
    return np.tile(idx.reshape(-1, 16).T, (8, 1)).astype(np.uint16)


def unstriped(offs):
    return offs[:16].T.reshape(-1).astype(np.int64)


def planes(y):
    n, m = y.shape
    v = y.astype(np.float32).astype(ml_dtypes.bfloat16).astype(np.float64).reshape(n // 32, 32, m)
    top = np.abs(v).max(1)
    byte = np.clip(np.where(top > 0, np.frexp(top)[1] - 1 + 127 - 7, 1), 1, 254)
    codes = (v * np.exp2(127.0 - byte)[:, None, :]).reshape(n, m).astype(np.float32).astype(ml_dtypes.float8_e4m3fn).view(np.uint8)
    words = codes.reshape(n // 512, 128, 4, m).transpose(0, 1, 3, 2)
    return np.ascontiguousarray(words), np.ascontiguousarray(byte.astype(np.uint8).reshape(n // 512, 16, m))


K, N, T, J = 512, 512, 2048, 1024


def setup_inputs():
    n = np.random.standard_normal
    s = mx_kscale(K)[:, None]
    m = np.exp(0.5 * n((1, J)))
    return {
        "dy": (m * n((K, J)) * s).astype(np.float32),
        "w": (n((K, N)) / np.sqrt(K) / s).astype(np.float32),
        "res": (n((N, J))).astype(np.float32),
        "wgo": np.tile(np.random.uniform(0.5, 2.0, J), (128, 1)).astype(np.float32),
        "offs": striped(np.random.permutation(T)[:J]),
    }


def reference(dy, w, res, wgo, offs):
    idx = unstriped(offs)
    dy_q_ = mxq(f64(dy), 0, "e5m2")
    dy_r_ = mxq(f64(dy) - dy_q_, 0, "e4m3")
    w_ = mxq(f64(w), 0, "e4m3")
    dx = w_.T @ dy_q_ + w_.T @ dy_r_
    out = np.zeros((N, T))
    out[:, idx] = f64(wgo)[0] * (dx + f64(res))
    return (out,) + planes(out)

@@ -1,0 +1,239 @@
+from contextlib import ExitStack
+
+import concourse.mybir as mybir
+from concourse.masks import make_identity
+
+K, N, T, J = 512, 512, 2048, 1024
+FLOPS = 3 * 2 * K * N * J
+
+F32 = mybir.dt.float32
+BF16 = mybir.dt.bfloat16
+U32 = mybir.dt.uint32
+I32 = mybir.dt.int32
+U16 = mybir.dt.uint16
+U8 = mybir.dt.uint8
+E4M3 = mybir.dt.float8_e4m3fn_x4
+E5M2 = mybir.dt.float8_e5m2_x4
+ADD = mybir.AluOpType.add
+SUB = mybir.AluOpType.subtract
+MULT = mybir.AluOpType.mult
+
+P = 128
+PACK = 4
+CHUNK = 256
+HALF = 512
+BACK = 128
+RUN = 4
+SPLIT = 768
+TQ = 256
+
+
+def flat(tile):
+    return tile[:].rearrange("p c i -> p (c i)")
+
+
+def tile_list_embg_tgf32_resP_kernel(tc, dy, w, res, wgo, offs, out_0, out_1, out_2):
+    nc = tc.nc
+    chunks = J // CHUNK
+    halves = J // HALF
+    with ExitStack() as ctx:
+        keep = ctx.enter_context(tc.tile_pool(name="keep", bufs=1))
+        psum = ctx.enter_context(tc.psum_pool(name="psum", bufs=4))
+
+        offsets = keep.tile([P, J // 16], U16, name="offsets")
+        dy_rows = dy.rearrange("(p i) j -> p i j", i=PACK)
+        w_rows = w.rearrange("(p i) n -> p i n", i=PACK)
+        res_rows = res.rearrange("(p i) j -> p i j", i=PACK)
+        out_rows = out_0.rearrange("(p i) t -> p i t", i=PACK)
+
+        dy_raw = [keep.tile([P, PACK, CHUNK], F32, name="dy_raw%d" % c, tag="raw%d" % c, align_bytes=64) for c in range(chunks)]
+        w_raw = [keep.tile([P, PACK, N // 2], F32, name="w_raw%d" % h) for h in range(2)]
+        res_sb = [[keep.tile([P, HALF], F32, name="res%d_%d" % (i, h)) for h in range(halves)] for i in range(PACK)]
+        wgo_sb = [keep.tile([P, HALF], F32, name="wgo%d" % h) for h in range(halves)]
+
+        def load_dy(c):
+            nc.sync.dma_start(out=dy_raw[c][:], in_=dy_rows[:, :, c * CHUNK : (c + 1) * CHUNK])
+
+        def load_res(i, h):
+            nc.sync.dma_start(out=res_sb[i][h][:], in_=res_rows[:, i, h * HALF : (h + 1) * HALF])
+
+        def load_wgo(h):
+            nc.sync.dma_start(out=wgo_sb[h][:], in_=wgo[:, h * HALF : (h + 1) * HALF])
+
+        load_dy(0)
+        load_dy(1)
+        for h in range(2):
+            nc.sync.dma_start(out=w_raw[h][:], in_=w_rows[:, :, h * (N // 2) : (h + 1) * (N // 2)])
+        load_dy(2)
+        load_dy(3)
+        load_res(0, 0)
+        nc.sync.dma_start(offsets[:], offs)
+        load_wgo(0)
+        load_res(1, 0)
+        load_res(0, 1)
+        load_wgo(1)
+        load_res(1, 1)
+        for i in (2, 3):
+            for h in range(halves):
+                load_res(i, h)
+
+        eye = keep.tile([P, P], BF16, name="eye")
+        make_identity(nc, eye[:])
+        eye_grouped = keep.tile([P, PACK * (K + 1)], BF16, name="eye_grouped", tag="grouped0", align_bytes=64)
+        nc.vector.memset(eye_grouped[:].bitcast(I32), 0)
+        nc.vector.tensor_copy(
+            out=eye_grouped[:].rearrange("p (i x) -> p i x", i=PACK)[:, :, 0 : K : PACK],
+            in_=eye[:].unsqueeze(1).to_broadcast([P, PACK, P]))
+        eye_codes = keep.tile([P, K], U32, name="eye_codes", align_bytes=64)
+        eye_scales = keep.tile([P, K], U8, name="eye_scales", align_bytes=64)
+        nc.vector.quantize_mx(
+            out=eye_codes[:].bitcast(E4M3), scales=eye_scales[:],
+            in_=eye_grouped[:, 0 : PACK * K])
+
+        pages = [None] * PACK
+
+        q_codes = [keep.tile([P, HALF], U32, name="q_codes0", align_bytes=64), None]
+        q_scales = [keep.tile([P, HALF], U8, name="q_scales%d" % h, align_bytes=64) for h in range(halves)]
+        r_codes = [keep.tile([P, HALF], U32, name="r_codes%d" % h, align_bytes=64) for h in range(halves)]
+        r_scales = [keep.tile([P, HALF], U8, name="r_scales%d" % h, align_bytes=64) for h in range(halves)]
+        w_scales = keep.tile([P, N], U8, name="w_scales", align_bytes=64)
+        left = [None] * chunks
+        sums = {}
+
+        def place(c):
+            h, part = divmod(c, HALF // CHUNK)
+            return h, part * CHUNK
+
+        def first_tier(c):
+            h, at = place(c)
+            grouped = keep.tile([P, CHUNK, PACK], BF16, name="dy_grouped%d" % c, tag="page0" if c == 1 else "grouped%d" % c, align_bytes=64)
+            copy = nc.vector.tensor_copy if h == 0 else nc.scalar.copy
+            copy(out=grouped[:].rearrange("p (c r) i -> p c i r", r=RUN),
+                 in_=dy_raw[c][:].rearrange("p i (c r) -> p c i r", r=RUN))
+            nc.vector.quantize_mx(out=q_codes[h][:, at : at + CHUNK].bitcast(E5M2),
+                                  scales=q_scales[h][:, at : at + CHUNK], in_=flat(grouped))
+
+        def leftover(c):
+            h, at = place(c)
+            tag = "page1" if c == chunks - 1 else "left%d" % c
+            left[c] = keep.tile([P, CHUNK, PACK], BF16, name="left%d" % c, tag=tag, align_bytes=64)
+            for b in range(CHUNK // BACK):
+                cols = slice(at + b * BACK, at + (b + 1) * BACK)
+                local = slice(b * BACK, (b + 1) * BACK)
+                back = psum.tile([P, PACK, BACK], F32, name="back")
+                for i in range(PACK):
+                    nc.tensor.matmul_mx(
+                        out=back[:, i, :],
+                        lhsT=eye_codes[:, i * P : (i + 1) * P].bitcast(E4M3),
+                        lhsT_scale=eye_scales[:, i * P : (i + 1) * P],
+                        rhs=q_codes[h][:, cols].bitcast(E5M2), rhs_scale=q_scales[h][:, cols],
+                        start=True, stop=True)
+                nc.vector.tensor_tensor(
+                    out=left[c][:, local, :].rearrange("p (c r) i -> p c i r", r=RUN),
+                    in0=dy_raw[c][:, :, local].rearrange("p i (c r) -> p c i r", r=RUN),
+                    in1=back[:].rearrange("p i (c r) -> p c i r", r=RUN), op=SUB)
+
+        def second_tier(c):
+            h, at = place(c)
+            nc.vector.quantize_mx(out=r_codes[h][:, at : at + CHUNK].bitcast(E4M3),
+                                  scales=r_scales[h][:, at : at + CHUNK], in_=flat(left[c]))
+
+        def quantize_w():
+            grouped = keep.tile([P, PACK, P, PACK], BF16, name="w_grouped", tag="w_grouped", align_bytes=64)
+            for h in range(2):
+                nc.scalar.copy(
+                    out=grouped[:, :, h * (P // 2) : (h + 1) * (P // 2), :].rearrange("p i m b -> p m b i"),
+                    in_=w_raw[h][:].rearrange("p b (m i) -> p m b i", i=PACK))
+            codes = keep.tile([P, N], U32, name="w_codes", tag="raw1", align_bytes=64)
+            nc.vector.quantize_mx(out=codes[:].bitcast(E4M3), scales=w_scales[:],
+                                  in_=grouped[:].rearrange("p i m b -> p (i m b)"))
+            return codes
+
+        def add_residual(i, h):
+            acc = psum.tile([P, HALF], F32, name="acc")
+            cols = slice(i * P, (i + 1) * P)
+            nc.tensor.matmul_mx(out=acc[:], lhsT=w_codes[:, cols].bitcast(E4M3), lhsT_scale=w_scales[:, cols],
+                                rhs=q_codes[h][:].bitcast(E5M2), rhs_scale=q_scales[h][:], start=True, stop=False)
+            nc.tensor.matmul_mx(out=acc[:], lhsT=w_codes[:, cols].bitcast(E4M3), lhsT_scale=w_scales[:, cols],
+                                rhs=r_codes[h][:].bitcast(E4M3), rhs_scale=r_scales[h][:], start=False, stop=True)
+            tag = "page%d" % (i + 1) if (h == 0 and 1 <= i < PACK - 1) else "sum%d_%d" % (i, h)
+            sums[i, h] = keep.tile([P, HALF], F32, name="sum%d_%d" % (i, h), tag=tag, align_bytes=64)
+            if (i, h) == (PACK - 1, halves - 1):
+                dx = keep.tile([P, HALF], F32, name="dx_last", tag="sum%d_%d" % (i - 1, h), align_bytes=64)
+                nc.scalar.copy(out=dx[:], in_=acc[:])
+                acc = dx
+            nc.vector.tensor_tensor(out=sums[i, h][:], in0=acc[:], in1=res_sb[i][h][:], op=ADD)
+
+        def clear_page(i):
+            pages[i] = keep.tile([P, T], F32, name="page%d" % i, tag="page%d" % i, align_bytes=64)
+            nc.gpsimd.memset(pages[i][:], 0.0)
+
+        def scatter(i, h):
+            listed = offsets[:, h * (HALF // 16) : (h + 1) * (HALF // 16)]
+            nc.vector.tensor_tensor(out=pages[i][:].indirect(listed), in0=sums[i, h][:], in1=wgo_sb[h][:], op=MULT)
+
+        out_grouped = keep.tile([P, T, PACK], BF16, name="out_grouped", align_bytes=64)
+
+        def store_page(i):
+            nc.sync.dma_start(out=out_rows[:, i, :], in_=pages[i][:])
+
+        first_tier(0)
+        first_tier(1)
+        clear_page(0)
+        leftover(0)
+        leftover(1)
+        second_tier(0)
+        w_codes = quantize_w()
+        second_tier(1)
+        q_codes[1] = keep.tile([P, HALF], U32, name="q_codes1", tag="w_grouped", align_bytes=64)
+        first_tier(2)
+        first_tier(3)
+        add_residual(0, 0)
+        scatter(0, 0)
+        add_residual(1, 0)
+        leftover(2)
+        leftover(3)
+        second_tier(2)
+        second_tier(3)
+        clear_page(1)
+        add_residual(0, 1)
+        add_residual(1, 1)
+        scatter(0, 1)
+        store_page(0)
+        nc.scalar.copy(out=out_grouped[:, :, 0], in_=pages[0][:])
+        last = PACK - 1
+        for i in range(1, last):
+            scatter(i, 0)
+            clear_page(i + 1)
+            add_residual(i + 1, 0)
+            if i + 1 < last:
+                add_residual(i + 1, 1)
+            scatter(i, 1)
+            store_page(i)
+            if i + 1 < last:
+                nc.scalar.copy(out=out_grouped[:, :, i], in_=pages[i][:])
+        nc.scalar.copy(out=out_grouped[:, :SPLIT, last - 1], in_=pages[last - 1][:, :SPLIT])
+        scatter(last, 0)
+        add_residual(last, 1)
+        nc.scalar.copy(out=out_grouped[:, SPLIT:, last - 1], in_=pages[last - 1][:, SPLIT:])
+        scatter(last, 1)
+        store_page(last)
+
+        y_codes = keep.tile([P, T], U32, name="y_codes", align_bytes=64)
+        y_scales = keep.tile([P, T], U8, name="y_scales", align_bytes=64)
+        words = out_1[0].rearrange("p t i -> p (t i)").bitcast(I32)
+        nc.vector.tensor_copy(out=out_grouped[:, :SPLIT, last], in_=pages[last][:, :SPLIT])
+        for g in range(SPLIT // TQ, T // TQ):
+            cols = slice(g * TQ, (g + 1) * TQ)
+            nc.scalar.copy(out=out_grouped[:, cols, last], in_=pages[last][:, cols])
+        for g in range(T // TQ):
+            cols = slice(g * TQ, (g + 1) * TQ)
+            nc.vector.quantize_mx(out=y_codes[:, cols].bitcast(E4M3), scales=y_scales[:, cols],
+                                  in_=out_grouped[:, cols, :].rearrange("p t i -> p (t i)"))
+            if g % 2 == 1:
+                cols = slice((g - 1) * TQ, (g + 1) * TQ)
+                nc.sync.dma_start(out=words[:, cols], in_=y_codes[:, cols].bitcast(I32))
+        for q in range(4):
+            queue = nc.sync if q % 2 == 0 else nc.scalar
+            queue.dma_start(out=out_2[0, 4 * q : 4 * q + 4, :].bitcast(I32),
+                            in_=y_scales[32 * q : 32 * q + 4, :].bitcast(I32))

@@ -48,7 +48,7 @@ def tile_list_embg_tgf32_resP_kernel(tc, dy, w, res, wgo, offs, out_0, out_1, ou
 
         dy_raw = [keep.tile([P, PACK, CHUNK], F32, name="dy_raw%d" % c, tag="raw%d" % c, align_bytes=64) for c in range(chunks)]
         w_raw = [keep.tile([P, PACK, N // 2], F32, name="w_raw%d" % h) for h in range(2)]
-        res_sb = [[keep.tile([P, HALF], F32, name="res%d_%d" % (i, h)) for h in range(halves)] for i in range(PACK)]
+        res_sb = [[keep.tile([P, HALF], F32, name="res%d_%d" % (i, h), tag="res%d" % (i * halves + h), align_bytes=64) for h in range(halves)] for i in range(PACK)]
         wgo_sb = [keep.tile([P, HALF], F32, name="wgo%d" % h) for h in range(halves)]
 
         def load_dy(c):
@@ -69,15 +69,13 @@ def tile_list_embg_tgf32_resP_kernel(tc, dy, w, res, wgo, offs, out_0, out_1, ou
         load_res(0, 0)
         nc.sync.dma_start(offsets[:], offs)
         load_wgo(0)
-        load_res(1, 0)
         load_res(0, 1)
         load_wgo(1)
-        load_res(1, 1)
-        for i in (2, 3):
+        for i in (1, 2, 3):
             for h in range(halves):
                 load_res(i, h)
 
-        eye = keep.tile([P, P], BF16, name="eye")
+        eye = keep.tile([P, P], BF16, name="eye", tag="page0", align_bytes=64)
         make_identity(nc, eye[:])
         eye_grouped = keep.tile([P, PACK * (K + 1)], BF16, name="eye_grouped", tag="grouped0", align_bytes=64)
         nc.vector.memset(eye_grouped[:].bitcast(I32), 0)
@@ -115,7 +113,7 @@ def tile_list_embg_tgf32_resP_kernel(tc, dy, w, res, wgo, offs, out_0, out_1, ou
 
         def leftover(c):
             h, at = place(c)
-            tag = "page1" if c == chunks - 1 else "left%d" % c
+            tag = "left%d" % c
             left[c] = keep.tile([P, CHUNK, PACK], BF16, name="left%d" % c, tag=tag, align_bytes=64)
             for b in range(CHUNK // BACK):
                 cols = slice(at + b * BACK, at + (b + 1) * BACK)
@@ -156,21 +154,24 @@ def tile_list_embg_tgf32_resP_kernel(tc, dy, w, res, wgo, offs, out_0, out_1, ou
                                 rhs=q_codes[h][:].bitcast(E5M2), rhs_scale=q_scales[h][:], start=True, stop=False)
             nc.tensor.matmul_mx(out=acc[:], lhsT=w_codes[:, cols].bitcast(E4M3), lhsT_scale=w_scales[:, cols],
                                 rhs=r_codes[h][:].bitcast(E4M3), rhs_scale=r_scales[h][:], start=False, stop=True)
-            tag = "page%d" % (i + 1) if (h == 0 and 1 <= i < PACK - 1) else "sum%d_%d" % (i, h)
-            sums[i, h] = keep.tile([P, HALF], F32, name="sum%d_%d" % (i, h), tag=tag, align_bytes=64)
-            if (i, h) == (PACK - 1, halves - 1):
-                dx = keep.tile([P, HALF], F32, name="dx_last", tag="sum%d_%d" % (i - 1, h), align_bytes=64)
-                nc.scalar.copy(out=dx[:], in_=acc[:])
-                acc = dx
-            nc.vector.tensor_tensor(out=sums[i, h][:], in0=acc[:], in1=res_sb[i][h][:], op=ADD)
+            step = i * halves + h
+            tag = "page%d" % (i + 1) if (h == 0 and i < PACK - 1) else "dx%d" % step
+            dx = keep.tile([P, HALF], F32, name="dx%d" % step, tag=tag, align_bytes=64)
+            nc.scalar.copy(out=dx[:], in_=acc[:])
+            tag = "res%d" % (step - 1) if step else "total0"
+            total = keep.tile([P, HALF], F32, name="total%d" % step, tag=tag, align_bytes=64)
+            nc.gpsimd.tensor_tensor(out=total[:], in0=dx[:], in1=res_sb[i][h][:], op=ADD)
+            sums[i, h] = keep.tile([P, HALF], F32, name="weighted%d" % step)
+            nc.gpsimd.tensor_tensor(out=sums[i, h][:], in0=total[:], in1=wgo_sb[h][:], op=MULT)
 
-        def clear_page(i):
+        def clear_page(i, pieces):
             pages[i] = keep.tile([P, T], F32, name="page%d" % i, tag="page%d" % i, align_bytes=64)
-            nc.gpsimd.memset(pages[i][:], 0.0)
+            for a in range(0, T, T // pieces):
+                nc.gpsimd.memset(pages[i][:, a : a + T // pieces], 0.0)
 
         def scatter(i, h):
             listed = offsets[:, h * (HALF // 16) : (h + 1) * (HALF // 16)]
-            nc.vector.tensor_tensor(out=pages[i][:].indirect(listed), in0=sums[i, h][:], in1=wgo_sb[h][:], op=MULT)
+            nc.vector.tensor_copy(out=pages[i][:].indirect(listed), in_=sums[i, h][:])
 
         out_grouped = keep.tile([P, T, PACK], BF16, name="out_grouped", align_bytes=64)
 
@@ -179,7 +180,7 @@ def tile_list_embg_tgf32_resP_kernel(tc, dy, w, res, wgo, offs, out_0, out_1, ou
 
         first_tier(0)
         first_tier(1)
-        clear_page(0)
+        clear_page(0, 1)
         leftover(0)
         leftover(1)
         second_tier(0)
@@ -189,40 +190,31 @@ def tile_list_embg_tgf32_resP_kernel(tc, dy, w, res, wgo, offs, out_0, out_1, ou
         first_tier(2)
         first_tier(3)
         add_residual(0, 0)
-        scatter(0, 0)
-        add_residual(1, 0)
         leftover(2)
         leftover(3)
         second_tier(2)
         second_tier(3)
-        clear_page(1)
-        add_residual(0, 1)
-        add_residual(1, 1)
-        scatter(0, 1)
-        store_page(0)
-        nc.scalar.copy(out=out_grouped[:, :, 0], in_=pages[0][:])
         last = PACK - 1
-        for i in range(1, last):
+        staged = keep.tile([P, 2, SPLIT], BF16, name="staged", align_bytes=64)
+        for i in range(PACK):
+            add_residual(i, 1)
             scatter(i, 0)
-            clear_page(i + 1)
-            add_residual(i + 1, 0)
-            if i + 1 < last:
-                add_residual(i + 1, 1)
+            if i < last:
+                add_residual(i + 1, 0)
+                clear_page(i + 1, 4)
             scatter(i, 1)
             store_page(i)
-            if i + 1 < last:
+            if i < last - 1:
                 nc.scalar.copy(out=out_grouped[:, :, i], in_=pages[i][:])
-        nc.scalar.copy(out=out_grouped[:, :SPLIT, last - 1], in_=pages[last - 1][:, :SPLIT])
-        scatter(last, 0)
-        add_residual(last, 1)
-        nc.scalar.copy(out=out_grouped[:, SPLIT:, last - 1], in_=pages[last - 1][:, SPLIT:])
-        scatter(last, 1)
-        store_page(last)
+            if i == last - 1:
+                nc.scalar.copy(out=staged[:, 0, :], in_=pages[i][:, :SPLIT])
+                nc.scalar.copy(out=out_grouped[:, SPLIT:, i], in_=pages[i][:, SPLIT:])
 
         y_codes = keep.tile([P, T], U32, name="y_codes", align_bytes=64)
         y_scales = keep.tile([P, T], U8, name="y_scales", align_bytes=64)
         words = out_1[0].rearrange("p t i -> p (t i)").bitcast(I32)
-        nc.vector.tensor_copy(out=out_grouped[:, :SPLIT, last], in_=pages[last][:, :SPLIT])
+        nc.vector.tensor_copy(out=staged[:, 1, :], in_=pages[last][:, :SPLIT])
+        nc.vector.tensor_copy(out=out_grouped[:, :SPLIT, last - 1 :], in_=staged[:].rearrange("p i t -> p t i"))
         for g in range(SPLIT // TQ, T // TQ):
             cols = slice(g * TQ, (g + 1) * TQ)
             nc.scalar.copy(out=out_grouped[:, cols, last], in_=pages[last][:, cols])

@@ -24,8 +24,9 @@ CHUNK = 256
 HALF = 512
 BACK = 128
 RUN = 4
-SPLIT = 768
-TQ = 256
+SPLIT = 896
+VECTOR_PARTS = (512, 384)
+SCALAR_PARTS = (384, 384, 256, 128)
 
 
 def flat(tile):
@@ -38,7 +39,7 @@ def tile_list_embg_tgf32_resP_kernel(tc, dy, w, res, wgo, offs, out_0, out_1, ou
     halves = J // HALF
     with ExitStack() as ctx:
         keep = ctx.enter_context(tc.tile_pool(name="keep", bufs=1))
-        psum = ctx.enter_context(tc.psum_pool(name="psum", bufs=4))
+        psum = ctx.enter_context(tc.psum_pool(name="psum", bufs=1))
 
         offsets = keep.tile([P, J // 16], U16, name="offsets")
         dy_rows = dy.rearrange("(p i) j -> p i j", i=PACK)
@@ -47,8 +48,8 @@ def tile_list_embg_tgf32_resP_kernel(tc, dy, w, res, wgo, offs, out_0, out_1, ou
         out_rows = out_0.rearrange("(p i) t -> p i t", i=PACK)
 
         dy_raw = [keep.tile([P, PACK, CHUNK], F32, name="dy_raw%d" % c, tag="raw%d" % c, align_bytes=64) for c in range(chunks)]
-        w_raw = [keep.tile([P, PACK, N // 2], F32, name="w_raw%d" % h) for h in range(2)]
-        res_sb = [[keep.tile([P, HALF], F32, name="res%d_%d" % (i, h), tag="res%d" % (i * halves + h), align_bytes=64) for h in range(halves)] for i in range(PACK)]
+        w_raw = [keep.tile([P, PACK, N // 2], F32, name="w_raw%d" % h, tag="grouped%d" % (2 + h), align_bytes=64) for h in range(2)]
+        res_sb = [[keep.tile([P, HALF], F32, name="res%d_%d" % (i, h), tag="page1" if i + h == 0 else "res%d" % (i * halves + h), align_bytes=64) for h in range(halves)] for i in range(PACK)]
         wgo_sb = [keep.tile([P, HALF], F32, name="wgo%d" % h) for h in range(halves)]
 
         def load_dy(c):
@@ -66,37 +67,42 @@ def tile_list_embg_tgf32_resP_kernel(tc, dy, w, res, wgo, offs, out_0, out_1, ou
             nc.sync.dma_start(out=w_raw[h][:], in_=w_rows[:, :, h * (N // 2) : (h + 1) * (N // 2)])
         load_dy(2)
         load_dy(3)
+        load_res(1, 0)
+        load_wgo(0)
         load_res(0, 0)
         nc.sync.dma_start(offsets[:], offs)
-        load_wgo(0)
         load_res(0, 1)
         load_wgo(1)
-        for i in (1, 2, 3):
+        load_res(1, 1)
+        for i in (2, 3):
             for h in range(halves):
                 load_res(i, h)
 
-        eye = keep.tile([P, P], BF16, name="eye", tag="page0", align_bytes=64)
+        eye = keep.tile([P, P], BF16, name="eye")
         make_identity(nc, eye[:])
-        eye_grouped = keep.tile([P, PACK * (K + 1)], BF16, name="eye_grouped", tag="grouped0", align_bytes=64)
-        nc.vector.memset(eye_grouped[:].bitcast(I32), 0)
-        nc.vector.tensor_copy(
-            out=eye_grouped[:].rearrange("p (i x) -> p i x", i=PACK)[:, :, 0 : K : PACK],
-            in_=eye[:].unsqueeze(1).to_broadcast([P, PACK, P]))
         eye_codes = keep.tile([P, K], U32, name="eye_codes", align_bytes=64)
         eye_scales = keep.tile([P, K], U8, name="eye_scales", align_bytes=64)
-        nc.vector.quantize_mx(
-            out=eye_codes[:].bitcast(E4M3), scales=eye_scales[:],
-            in_=eye_grouped[:, 0 : PACK * K])
+        for u, tag in enumerate(("page3", "page0")):
+            grouped = keep.tile([P, 2 * (K + 2)], BF16, name="eye_grouped%d" % u, tag=tag, align_bytes=64)
+            nc.vector.memset(grouped[:].bitcast(I32), 0)
+            ones = grouped[:, 2 * u : 2 * u + 2 * (K + 1)].rearrange("p (i x) -> p i x", i=2)[:, :, 0 : K : PACK]
+            copy = nc.scalar.copy if u else nc.vector.tensor_copy
+            copy(out=ones, in_=eye[:].unsqueeze(1).to_broadcast([P, 2, P]))
+            cols = slice(2 * u * P, 2 * (u + 1) * P)
+            nc.vector.quantize_mx(out=eye_codes[:, cols].bitcast(E4M3), scales=eye_scales[:, cols],
+                                  in_=grouped[:, 0 : 2 * K])
 
         pages = [None] * PACK
 
         q_codes = [keep.tile([P, HALF], U32, name="q_codes0", align_bytes=64), None]
         q_scales = [keep.tile([P, HALF], U8, name="q_scales%d" % h, align_bytes=64) for h in range(halves)]
-        r_codes = [keep.tile([P, HALF], U32, name="r_codes%d" % h, align_bytes=64) for h in range(halves)]
+        r_codes = [keep.tile([P, HALF], U32, name="r_codes%d" % h, tag="page2" if h else "r_codes0", align_bytes=64)
+                   for h in range(halves)]
         r_scales = [keep.tile([P, HALF], U8, name="r_scales%d" % h, align_bytes=64) for h in range(halves)]
         w_scales = keep.tile([P, N], U8, name="w_scales", align_bytes=64)
         left = [None] * chunks
         sums = {}
+        dx = {}
 
         def place(c):
             h, part = divmod(c, HALF // CHUNK)
@@ -104,8 +110,8 @@ def tile_list_embg_tgf32_resP_kernel(tc, dy, w, res, wgo, offs, out_0, out_1, ou
 
         def first_tier(c):
             h, at = place(c)
-            grouped = keep.tile([P, CHUNK, PACK], BF16, name="dy_grouped%d" % c, tag="page0" if c == 1 else "grouped%d" % c, align_bytes=64)
-            copy = nc.vector.tensor_copy if h == 0 else nc.scalar.copy
+            grouped = keep.tile([P, CHUNK, PACK], BF16, name="dy_grouped%d" % c, tag=("page3", "page0", "grouped2", "grouped3")[c], align_bytes=64)
+            copy = nc.vector.tensor_copy if c == 0 else nc.scalar.copy
             copy(out=grouped[:].rearrange("p (c r) i -> p c i r", r=RUN),
                  in_=dy_raw[c][:].rearrange("p i (c r) -> p c i r", r=RUN))
             nc.vector.quantize_mx(out=q_codes[h][:, at : at + CHUNK].bitcast(E5M2),
@@ -118,7 +124,7 @@ def tile_list_embg_tgf32_resP_kernel(tc, dy, w, res, wgo, offs, out_0, out_1, ou
             for b in range(CHUNK // BACK):
                 cols = slice(at + b * BACK, at + (b + 1) * BACK)
                 local = slice(b * BACK, (b + 1) * BACK)
-                back = psum.tile([P, PACK, BACK], F32, name="back")
+                back = psum.tile([P, PACK, BACK], F32, name="back", bufs=3)
                 for i in range(PACK):
                     nc.tensor.matmul_mx(
                         out=back[:, i, :],
@@ -127,9 +133,9 @@ def tile_list_embg_tgf32_resP_kernel(tc, dy, w, res, wgo, offs, out_0, out_1, ou
                         rhs=q_codes[h][:, cols].bitcast(E5M2), rhs_scale=q_scales[h][:, cols],
                         start=True, stop=True)
                 nc.vector.tensor_tensor(
-                    out=left[c][:, local, :].rearrange("p (c r) i -> p c i r", r=RUN),
-                    in0=dy_raw[c][:, :, local].rearrange("p i (c r) -> p c i r", r=RUN),
-                    in1=back[:].rearrange("p i (c r) -> p c i r", r=RUN), op=SUB)
+                    out=left[c][:, local, :].rearrange("p (c r) i -> p c i r", r=2),
+                    in0=dy_raw[c][:, :, local].rearrange("p i (c r) -> p c i r", r=2),
+                    in1=back[:].rearrange("p i (c r) -> p c i r", r=2), op=SUB)
 
         def second_tier(c):
             h, at = place(c)
@@ -137,7 +143,7 @@ def tile_list_embg_tgf32_resP_kernel(tc, dy, w, res, wgo, offs, out_0, out_1, ou
                                   scales=r_scales[h][:, at : at + CHUNK], in_=flat(left[c]))
 
         def quantize_w():
-            grouped = keep.tile([P, PACK, P, PACK], BF16, name="w_grouped", tag="w_grouped", align_bytes=64)
+            grouped = keep.tile([P, PACK, P, PACK], BF16, name="w_grouped", tag="page3", align_bytes=64)
             for h in range(2):
                 nc.scalar.copy(
                     out=grouped[:, :, h * (P // 2) : (h + 1) * (P // 2), :].rearrange("p i m b -> p m b i"),
@@ -147,31 +153,42 @@ def tile_list_embg_tgf32_resP_kernel(tc, dy, w, res, wgo, offs, out_0, out_1, ou
                                   in_=grouped[:].rearrange("p i m b -> p (i m b)"))
             return codes
 
-        def add_residual(i, h):
-            acc = psum.tile([P, HALF], F32, name="acc")
+        def product(i, h):
+            acc = psum.tile([P, HALF], F32, name="acc", bufs=5)
             cols = slice(i * P, (i + 1) * P)
             nc.tensor.matmul_mx(out=acc[:], lhsT=w_codes[:, cols].bitcast(E4M3), lhsT_scale=w_scales[:, cols],
                                 rhs=q_codes[h][:].bitcast(E5M2), rhs_scale=q_scales[h][:], start=True, stop=False)
             nc.tensor.matmul_mx(out=acc[:], lhsT=w_codes[:, cols].bitcast(E4M3), lhsT_scale=w_scales[:, cols],
                                 rhs=r_codes[h][:].bitcast(E4M3), rhs_scale=r_scales[h][:], start=False, stop=True)
+            if i == 0:
+                dx[i, h] = acc
+            else:
+                dx[i, h] = keep.tile([P, HALF], F32, name="dx%d_%d" % (i, h))
+                nc.scalar.copy(out=dx[i, h][:], in_=acc[:])
+
+        def add_on_vector(h):
+            tag = "left%d" % (chunks - 1)
+            sums[0, h] = keep.tile([P, HALF], F32, name="total0_%d" % h, tag=tag if h == 0 else "sum01", align_bytes=64)
+            nc.vector.tensor_tensor(out=sums[0, h][:], in0=dx[0, h][:], in1=res_sb[0][h][:], op=ADD)
+
+        def weigh_on_gpsimd(i, h):
             step = i * halves + h
-            tag = "page%d" % (i + 1) if (h == 0 and i < PACK - 1) else "dx%d" % step
-            dx = keep.tile([P, HALF], F32, name="dx%d" % step, tag=tag, align_bytes=64)
-            nc.scalar.copy(out=dx[:], in_=acc[:])
-            tag = "res%d" % (step - 1) if step else "total0"
+            tag = {2: "total2", 3: "sum01"}.get(step, "res%d" % (step - 1))
             total = keep.tile([P, HALF], F32, name="total%d" % step, tag=tag, align_bytes=64)
-            nc.gpsimd.tensor_tensor(out=total[:], in0=dx[:], in1=res_sb[i][h][:], op=ADD)
+            nc.gpsimd.tensor_tensor(out=total[:], in0=dx[i, h][:], in1=res_sb[i][h][:], op=ADD)
             sums[i, h] = keep.tile([P, HALF], F32, name="weighted%d" % step)
             nc.gpsimd.tensor_tensor(out=sums[i, h][:], in0=total[:], in1=wgo_sb[h][:], op=MULT)
 
-        def clear_page(i, pieces):
+        def clear_page(i):
             pages[i] = keep.tile([P, T], F32, name="page%d" % i, tag="page%d" % i, align_bytes=64)
-            for a in range(0, T, T // pieces):
-                nc.gpsimd.memset(pages[i][:, a : a + T // pieces], 0.0)
+            nc.gpsimd.memset(pages[i][:], 0.0)
 
         def scatter(i, h):
             listed = offsets[:, h * (HALF // 16) : (h + 1) * (HALF // 16)]
-            nc.vector.tensor_copy(out=pages[i][:].indirect(listed), in_=sums[i, h][:])
+            if i == 0:
+                nc.vector.tensor_tensor(out=pages[i][:].indirect(listed), in0=sums[i, h][:], in1=wgo_sb[h][:], op=MULT)
+            else:
+                nc.vector.tensor_copy(out=pages[i][:].indirect(listed), in_=sums[i, h][:])
 
         out_grouped = keep.tile([P, T, PACK], BF16, name="out_grouped", align_bytes=64)
 
@@ -180,51 +197,67 @@ def tile_list_embg_tgf32_resP_kernel(tc, dy, w, res, wgo, offs, out_0, out_1, ou
 
         first_tier(0)
         first_tier(1)
-        clear_page(0, 1)
+        clear_page(0)
         leftover(0)
         leftover(1)
         second_tier(0)
         w_codes = quantize_w()
-        second_tier(1)
-        q_codes[1] = keep.tile([P, HALF], U32, name="q_codes1", tag="w_grouped", align_bytes=64)
+        q_codes[1] = keep.tile([P, HALF], U32, name="q_codes1", tag="page3", align_bytes=64)
         first_tier(2)
+        second_tier(1)
         first_tier(3)
-        add_residual(0, 0)
+        product(1, 0)
+        weigh_on_gpsimd(1, 0)
         leftover(2)
         leftover(3)
+        for i in (0, 2, 3):
+            product(i, 0)
         second_tier(2)
         second_tier(3)
-        last = PACK - 1
-        staged = keep.tile([P, 2, SPLIT], BF16, name="staged", align_bytes=64)
+        add_on_vector(0)
         for i in range(PACK):
-            add_residual(i, 1)
+            product(i, 1)
+        for i in range(1, PACK):
+            clear_page(i)
+        add_on_vector(1)
+        last = PACK - 1
+        rounded = keep.tile([P, PACK, T], BF16, name="rounded", align_bytes=64)
+
+        def weave(copy, cols, planes):
+            copy(out=out_grouped[:, cols, planes].rearrange("p (c r) i -> p c i r", r=2),
+                 in_=rounded[:, planes, cols].rearrange("p i (c r) -> p c i r", r=2))
+
+        for i in range(PACK):
             scatter(i, 0)
-            if i < last:
-                add_residual(i + 1, 0)
-                clear_page(i + 1, 4)
+            if i > 0:
+                weigh_on_gpsimd(i, 1)
             scatter(i, 1)
+            if 0 < i < last:
+                weigh_on_gpsimd(i + 1, 0)
             store_page(i)
-            if i < last - 1:
-                nc.scalar.copy(out=out_grouped[:, :, i], in_=pages[i][:])
-            if i == last - 1:
-                nc.scalar.copy(out=staged[:, 0, :], in_=pages[i][:, :SPLIT])
-                nc.scalar.copy(out=out_grouped[:, SPLIT:, i], in_=pages[i][:, SPLIT:])
+            if i < last:
+                nc.scalar.copy(out=rounded[:, i, :], in_=pages[i][:])
+            if i == 1:
+                weave(nc.scalar.copy, slice(0, SPLIT), slice(0, 2))
+            if i == 2:
+                weave(nc.scalar.copy, slice(SPLIT, T), slice(0, 3))
 
         y_codes = keep.tile([P, T], U32, name="y_codes", align_bytes=64)
         y_scales = keep.tile([P, T], U8, name="y_scales", align_bytes=64)
         words = out_1[0].rearrange("p t i -> p (t i)").bitcast(I32)
-        nc.vector.tensor_copy(out=staged[:, 1, :], in_=pages[last][:, :SPLIT])
-        nc.vector.tensor_copy(out=out_grouped[:, :SPLIT, last - 1 :], in_=staged[:].rearrange("p i t -> p t i"))
-        for g in range(SPLIT // TQ, T // TQ):
-            cols = slice(g * TQ, (g + 1) * TQ)
-            nc.scalar.copy(out=out_grouped[:, cols, last], in_=pages[last][:, cols])
-        for g in range(T // TQ):
-            cols = slice(g * TQ, (g + 1) * TQ)
+        nc.vector.tensor_copy(out=rounded[:, last, :SPLIT], in_=pages[last][:, :SPLIT])
+        weave(nc.vector.tensor_copy, slice(0, SPLIT), slice(2, 4))
+        at = SPLIT
+        for width in SCALAR_PARTS:
+            nc.scalar.copy(out=out_grouped[:, at : at + width, last], in_=pages[last][:, at : at + width])
+            at = at + width
+        at = 0
+        for width in VECTOR_PARTS + SCALAR_PARTS:
+            cols = slice(at, at + width)
             nc.vector.quantize_mx(out=y_codes[:, cols].bitcast(E4M3), scales=y_scales[:, cols],
                                   in_=out_grouped[:, cols, :].rearrange("p t i -> p (t i)"))
-            if g % 2 == 1:
-                cols = slice((g - 1) * TQ, (g + 1) * TQ)
-                nc.sync.dma_start(out=words[:, cols], in_=y_codes[:, cols].bitcast(I32))
+            nc.sync.dma_start(out=words[:, cols], in_=y_codes[:, cols].bitcast(I32))
+            at = at + width
         for q in range(4):
             queue = nc.sync if q % 2 == 0 else nc.scalar
             queue.dma_start(out=out_2[0, 4 * q : 4 * q + 4, :].bitcast(I32),

@@ -24,9 +24,10 @@ CHUNK = 256
 HALF = 512
 BACK = 128
 RUN = 4
-SPLIT = 896
-VECTOR_PARTS = (512, 384)
-SCALAR_PARTS = (384, 384, 256, 128)
+SPLIT = 768
+WOVEN = 1536
+VECTOR_PARTS = (384, 384)
+SCALAR_PARTS = (384, 384, 384, 128)
 
 
 def flat(tile):
@@ -48,8 +49,8 @@ def tile_list_embg_tgf32_resP_kernel(tc, dy, w, res, wgo, offs, out_0, out_1, ou
         out_rows = out_0.rearrange("(p i) t -> p i t", i=PACK)
 
         dy_raw = [keep.tile([P, PACK, CHUNK], F32, name="dy_raw%d" % c, tag="raw%d" % c, align_bytes=64) for c in range(chunks)]
-        w_raw = [keep.tile([P, PACK, N // 2], F32, name="w_raw%d" % h, tag="grouped%d" % (2 + h), align_bytes=64) for h in range(2)]
-        res_sb = [[keep.tile([P, HALF], F32, name="res%d_%d" % (i, h), tag="page1" if i + h == 0 else "res%d" % (i * halves + h), align_bytes=64) for h in range(halves)] for i in range(PACK)]
+        w_raw = [keep.tile([P, PACK, N // 2], F32, name="w_raw%d" % h, align_bytes=64) for h in range(2)]
+        res_sb = [[keep.tile([P, HALF], F32, name="res%d_%d" % (i, h), tag="page3" if i * halves + h == 3 else "res%d" % (i * halves + h), align_bytes=64) for h in range(halves)] for i in range(PACK)]
         wgo_sb = [keep.tile([P, HALF], F32, name="wgo%d" % h) for h in range(halves)]
 
         def load_dy(c):
@@ -61,20 +62,16 @@ def tile_list_embg_tgf32_resP_kernel(tc, dy, w, res, wgo, offs, out_0, out_1, ou
         def load_wgo(h):
             nc.sync.dma_start(out=wgo_sb[h][:], in_=wgo[:, h * HALF : (h + 1) * HALF])
 
-        load_dy(0)
-        load_dy(1)
+        for c in range(chunks):
+            load_dy(c)
         for h in range(2):
             nc.sync.dma_start(out=w_raw[h][:], in_=w_rows[:, :, h * (N // 2) : (h + 1) * (N // 2)])
-        load_dy(2)
-        load_dy(3)
-        load_res(1, 0)
-        load_wgo(0)
         load_res(0, 0)
         nc.sync.dma_start(offsets[:], offs)
+        load_wgo(0)
         load_res(0, 1)
         load_wgo(1)
-        load_res(1, 1)
-        for i in (2, 3):
+        for i in range(1, PACK):
             for h in range(halves):
                 load_res(i, h)
 
@@ -82,25 +79,21 @@ def tile_list_embg_tgf32_resP_kernel(tc, dy, w, res, wgo, offs, out_0, out_1, ou
         make_identity(nc, eye[:])
         eye_codes = keep.tile([P, K], U32, name="eye_codes", align_bytes=64)
         eye_scales = keep.tile([P, K], U8, name="eye_scales", align_bytes=64)
-        for u, tag in enumerate(("page3", "page0")):
-            grouped = keep.tile([P, 2 * (K + 2)], BF16, name="eye_grouped%d" % u, tag=tag, align_bytes=64)
-            nc.vector.memset(grouped[:].bitcast(I32), 0)
-            ones = grouped[:, 2 * u : 2 * u + 2 * (K + 1)].rearrange("p (i x) -> p i x", i=2)[:, :, 0 : K : PACK]
-            copy = nc.scalar.copy if u else nc.vector.tensor_copy
-            copy(out=ones, in_=eye[:].unsqueeze(1).to_broadcast([P, 2, P]))
-            cols = slice(2 * u * P, 2 * (u + 1) * P)
-            nc.vector.quantize_mx(out=eye_codes[:, cols].bitcast(E4M3), scales=eye_scales[:, cols],
-                                  in_=grouped[:, 0 : 2 * K])
+        eye_grouped = keep.tile([P, PACK * (K + 1)], BF16, name="eye_grouped", tag="first", align_bytes=64)
+        nc.vector.memset(eye_grouped[:].bitcast(I32), 0)
+        nc.vector.tensor_copy(out=eye_grouped[:].rearrange("p (i x) -> p i x", i=PACK)[:, :, 0:K:PACK],
+                              in_=eye[:].unsqueeze(1).to_broadcast([P, PACK, P]))
+        nc.vector.quantize_mx(out=eye_codes[:].bitcast(E4M3), scales=eye_scales[:], in_=eye_grouped[:, 0 : PACK * K])
 
         pages = [None] * PACK
 
-        q_codes = [keep.tile([P, HALF], U32, name="q_codes0", align_bytes=64), None]
+        q_codes = [None] * chunks
         q_scales = [keep.tile([P, HALF], U8, name="q_scales%d" % h, align_bytes=64) for h in range(halves)]
-        r_codes = [keep.tile([P, HALF], U32, name="r_codes%d" % h, tag="page2" if h else "r_codes0", align_bytes=64)
-                   for h in range(halves)]
+        r_codes = [None] * halves
         r_scales = [keep.tile([P, HALF], U8, name="r_scales%d" % h, align_bytes=64) for h in range(halves)]
         w_scales = keep.tile([P, N], U8, name="w_scales", align_bytes=64)
-        left = [None] * chunks
+        left = [keep.tile([P, HALF, PACK], BF16, name="left%d" % h, tag="page%d" % (1 + h), align_bytes=64)
+                for h in range(halves)]
         sums = {}
         dx = {}
 
@@ -108,76 +101,75 @@ def tile_list_embg_tgf32_resP_kernel(tc, dy, w, res, wgo, offs, out_0, out_1, ou
             h, part = divmod(c, HALF // CHUNK)
             return h, part * CHUNK
 
-        def first_tier(c):
-            h, at = place(c)
-            grouped = keep.tile([P, CHUNK, PACK], BF16, name="dy_grouped%d" % c, tag=("page3", "page0", "grouped2", "grouped3")[c], align_bytes=64)
+        def round_dy(c, grouped):
             copy = nc.vector.tensor_copy if c == 0 else nc.scalar.copy
-            copy(out=grouped[:].rearrange("p (c r) i -> p c i r", r=RUN),
+            copy(out=grouped.rearrange("p (c r) i -> p c i r", r=RUN),
                  in_=dy_raw[c][:].rearrange("p i (c r) -> p c i r", r=RUN))
-            nc.vector.quantize_mx(out=q_codes[h][:, at : at + CHUNK].bitcast(E5M2),
-                                  scales=q_scales[h][:, at : at + CHUNK], in_=flat(grouped))
+
+        def first_tier(c, grouped, codes):
+            h, at = place(c)
+            q_codes[c] = codes
+            nc.vector.quantize_mx(out=codes.bitcast(E5M2), scales=q_scales[h][:, at : at + CHUNK],
+                                  in_=grouped.rearrange("p c i -> p (c i)"))
 
         def leftover(c):
             h, at = place(c)
-            tag = "left%d" % c
-            left[c] = keep.tile([P, CHUNK, PACK], BF16, name="left%d" % c, tag=tag, align_bytes=64)
             for b in range(CHUNK // BACK):
                 cols = slice(at + b * BACK, at + (b + 1) * BACK)
                 local = slice(b * BACK, (b + 1) * BACK)
-                back = psum.tile([P, PACK, BACK], F32, name="back", bufs=3)
+                back = psum.tile([P, PACK, BACK], F32, name="back", bufs=4)
                 for i in range(PACK):
                     nc.tensor.matmul_mx(
                         out=back[:, i, :],
                         lhsT=eye_codes[:, i * P : (i + 1) * P].bitcast(E4M3),
                         lhsT_scale=eye_scales[:, i * P : (i + 1) * P],
-                        rhs=q_codes[h][:, cols].bitcast(E5M2), rhs_scale=q_scales[h][:, cols],
+                        rhs=q_codes[c][:, local].bitcast(E5M2), rhs_scale=q_scales[h][:, cols],
                         start=True, stop=True)
                 nc.vector.tensor_tensor(
-                    out=left[c][:, local, :].rearrange("p (c r) i -> p c i r", r=2),
+                    out=left[h][:, cols, :].rearrange("p (c r) i -> p c i r", r=2),
                     in0=dy_raw[c][:, :, local].rearrange("p i (c r) -> p c i r", r=2),
                     in1=back[:].rearrange("p i (c r) -> p c i r", r=2), op=SUB)
 
-        def second_tier(c):
-            h, at = place(c)
-            nc.vector.quantize_mx(out=r_codes[h][:, at : at + CHUNK].bitcast(E4M3),
-                                  scales=r_scales[h][:, at : at + CHUNK], in_=flat(left[c]))
+        def second_tier(h):
+            r_codes[h] = keep.tile([P, HALF], U32, name="r_codes%d" % h, tag=("grouped", "w_grouped")[h], align_bytes=64)
+            nc.vector.quantize_mx(out=r_codes[h][:].bitcast(E4M3), scales=r_scales[h][:], in_=flat(left[h]))
 
         def quantize_w():
-            grouped = keep.tile([P, PACK, P, PACK], BF16, name="w_grouped", tag="page3", align_bytes=64)
+            grouped = keep.tile([P, PACK, P, PACK], BF16, name="w_grouped", tag="w_grouped", align_bytes=64)
             for h in range(2):
                 nc.scalar.copy(
                     out=grouped[:, :, h * (P // 2) : (h + 1) * (P // 2), :].rearrange("p i m b -> p m b i"),
                     in_=w_raw[h][:].rearrange("p b (m i) -> p m b i", i=PACK))
-            codes = keep.tile([P, N], U32, name="w_codes", tag="raw1", align_bytes=64)
+            codes = keep.tile([P, N], U32, name="w_codes", tag="raw3", align_bytes=64)
             nc.vector.quantize_mx(out=codes[:].bitcast(E4M3), scales=w_scales[:],
                                   in_=grouped[:].rearrange("p i m b -> p (i m b)"))
             return codes
 
         def product(i, h):
-            acc = psum.tile([P, HALF], F32, name="acc", bufs=5)
+            acc = psum.tile([P, HALF], F32, name="acc", bufs=4)
             cols = slice(i * P, (i + 1) * P)
-            nc.tensor.matmul_mx(out=acc[:], lhsT=w_codes[:, cols].bitcast(E4M3), lhsT_scale=w_scales[:, cols],
-                                rhs=q_codes[h][:].bitcast(E5M2), rhs_scale=q_scales[h][:], start=True, stop=False)
-            nc.tensor.matmul_mx(out=acc[:], lhsT=w_codes[:, cols].bitcast(E4M3), lhsT_scale=w_scales[:, cols],
-                                rhs=r_codes[h][:].bitcast(E4M3), rhs_scale=r_scales[h][:], start=False, stop=True)
-            if i == 0:
+            weights = w_codes[:, cols].bitcast(E4M3)
+            nc.tensor.matmul_mx(out=acc[:], lhsT=weights, lhsT_scale=w_scales[:, cols],
+                                rhs=r_codes[h][:].bitcast(E4M3), rhs_scale=r_scales[h][:], start=True, stop=False)
+            for part in range(HALF // CHUNK):
+                local = slice(part * CHUNK, (part + 1) * CHUNK)
+                nc.tensor.matmul_mx(out=acc[:, local], lhsT=weights, lhsT_scale=w_scales[:, cols],
+                                    rhs=q_codes[h * (HALF // CHUNK) + part].bitcast(E5M2),
+                                    rhs_scale=q_scales[h][:, local], start=False, stop=(part == HALF // CHUNK - 1))
+            if i + h == 0:
                 dx[i, h] = acc
             else:
                 dx[i, h] = keep.tile([P, HALF], F32, name="dx%d_%d" % (i, h))
                 nc.scalar.copy(out=dx[i, h][:], in_=acc[:])
 
-        def add_on_vector(h):
-            tag = "left%d" % (chunks - 1)
-            sums[0, h] = keep.tile([P, HALF], F32, name="total0_%d" % h, tag=tag if h == 0 else "sum01", align_bytes=64)
-            nc.vector.tensor_tensor(out=sums[0, h][:], in0=dx[0, h][:], in1=res_sb[0][h][:], op=ADD)
-
-        def weigh_on_gpsimd(i, h):
+        def weigh(i, h):
             step = i * halves + h
-            tag = {2: "total2", 3: "sum01"}.get(step, "res%d" % (step - 1))
+            engine = nc.gpsimd if step else nc.vector
+            tag = {0: "total0", 1: "total1", 4: "page3"}.get(step, "res%d" % (step - 1))
             total = keep.tile([P, HALF], F32, name="total%d" % step, tag=tag, align_bytes=64)
-            nc.gpsimd.tensor_tensor(out=total[:], in0=dx[i, h][:], in1=res_sb[i][h][:], op=ADD)
+            engine.tensor_tensor(out=total[:], in0=dx[i, h][:], in1=res_sb[i][h][:], op=ADD)
             sums[i, h] = keep.tile([P, HALF], F32, name="weighted%d" % step)
-            nc.gpsimd.tensor_tensor(out=sums[i, h][:], in0=total[:], in1=wgo_sb[h][:], op=MULT)
+            engine.tensor_tensor(out=sums[i, h][:], in0=total[:], in1=wgo_sb[h][:], op=MULT)
 
         def clear_page(i):
             pages[i] = keep.tile([P, T], F32, name="page%d" % i, tag="page%d" % i, align_bytes=64)
@@ -185,68 +177,70 @@ def tile_list_embg_tgf32_resP_kernel(tc, dy, w, res, wgo, offs, out_0, out_1, ou
 
         def scatter(i, h):
             listed = offsets[:, h * (HALF // 16) : (h + 1) * (HALF // 16)]
-            if i == 0:
-                nc.vector.tensor_tensor(out=pages[i][:].indirect(listed), in0=sums[i, h][:], in1=wgo_sb[h][:], op=MULT)
-            else:
-                nc.vector.tensor_copy(out=pages[i][:].indirect(listed), in_=sums[i, h][:])
+            nc.vector.tensor_copy(out=pages[i][:].indirect(listed), in_=sums[i, h][:])
 
         out_grouped = keep.tile([P, T, PACK], BF16, name="out_grouped", align_bytes=64)
 
         def store_page(i):
             nc.sync.dma_start(out=out_rows[:, i, :], in_=pages[i][:])
 
-        first_tier(0)
-        first_tier(1)
+        grouped0 = keep.tile([P, CHUNK, PACK], BF16, name="dy_grouped0", tag="first", align_bytes=64)
+        round_dy(0, grouped0[:])
+        first_tier(0, grouped0[:], keep.tile([P, CHUNK], U32, name="q_codes0", align_bytes=64)[:])
+        grouped1 = keep.tile([P, CHUNK, PACK], BF16, name="dy_grouped1", tag="page0", align_bytes=64)
+        round_dy(1, grouped1[:])
+        first_tier(1, grouped1[:], keep.tile([P, CHUNK], U32, name="q_codes1", tag="first", align_bytes=64)[:])
         clear_page(0)
         leftover(0)
         leftover(1)
+        grouped23 = keep.tile([P, HALF, PACK], BF16, name="dy_grouped23", tag="grouped", align_bytes=64)
+        codes23 = keep.tile([P, HALF], U32, name="q_codes23", tag="raw1", align_bytes=64)
+        for part in range(2):
+            local = slice(part * CHUNK, (part + 1) * CHUNK)
+            round_dy(2 + part, grouped23[:, local, :])
+            first_tier(2 + part, grouped23[:, local, :], codes23[:, local])
         second_tier(0)
-        w_codes = quantize_w()
-        q_codes[1] = keep.tile([P, HALF], U32, name="q_codes1", tag="page3", align_bytes=64)
-        first_tier(2)
-        second_tier(1)
-        first_tier(3)
-        product(1, 0)
-        weigh_on_gpsimd(1, 0)
+        clear_page(1)
         leftover(2)
         leftover(3)
-        for i in (0, 2, 3):
-            product(i, 0)
-        second_tier(2)
-        second_tier(3)
-        add_on_vector(0)
+        w_codes = quantize_w()
+        second_tier(1)
         for i in range(PACK):
-            product(i, 1)
-        for i in range(1, PACK):
-            clear_page(i)
-        add_on_vector(1)
+            for h in range(halves):
+                product(i, h)
+        clear_page(2)
+        weigh(0, 0)
         last = PACK - 1
-        rounded = keep.tile([P, PACK, T], BF16, name="rounded", align_bytes=64)
+        staged = keep.tile([P, 2, SPLIT], BF16, name="staged", align_bytes=64)
+        waiting = keep.tile([P, last, T - WOVEN], BF16, name="waiting", align_bytes=64)
 
-        def weave(copy, cols, planes):
+        def weave(copy, cols, planes, rounded):
             copy(out=out_grouped[:, cols, planes].rearrange("p (c r) i -> p c i r", r=2),
-                 in_=rounded[:, planes, cols].rearrange("p i (c r) -> p c i r", r=2))
+                 in_=rounded[:].rearrange("p i (c r) -> p c i r", r=2))
 
         for i in range(PACK):
             scatter(i, 0)
-            if i > 0:
-                weigh_on_gpsimd(i, 1)
+            weigh(i, 1)
             scatter(i, 1)
-            if 0 < i < last:
-                weigh_on_gpsimd(i + 1, 0)
+            if i < last:
+                weigh(i + 1, 0)
+            if i == 1:
+                clear_page(last)
             store_page(i)
             if i < last:
-                nc.scalar.copy(out=rounded[:, i, :], in_=pages[i][:])
-            if i == 1:
-                weave(nc.scalar.copy, slice(0, SPLIT), slice(0, 2))
-            if i == 2:
-                weave(nc.scalar.copy, slice(SPLIT, T), slice(0, 3))
+                first = 0 if i < last - 1 else SPLIT
+                if first:
+                    nc.scalar.copy(out=staged[:, 0, :], in_=pages[i][:, :SPLIT])
+                nc.scalar.copy(out=waiting[:, i, :], in_=pages[i][:, WOVEN:])
+                nc.scalar.copy(out=out_grouped[:, first:WOVEN, i], in_=pages[i][:, first:WOVEN])
+                if first:
+                    weave(nc.scalar.copy, slice(WOVEN, T), slice(0, last), waiting)
 
         y_codes = keep.tile([P, T], U32, name="y_codes", align_bytes=64)
         y_scales = keep.tile([P, T], U8, name="y_scales", align_bytes=64)
         words = out_1[0].rearrange("p t i -> p (t i)").bitcast(I32)
-        nc.vector.tensor_copy(out=rounded[:, last, :SPLIT], in_=pages[last][:, :SPLIT])
-        weave(nc.vector.tensor_copy, slice(0, SPLIT), slice(2, 4))
+        nc.vector.tensor_copy(out=staged[:, 1, :], in_=pages[last][:, :SPLIT])
+        weave(nc.vector.tensor_copy, slice(0, SPLIT), slice(last - 1, PACK), staged)
         at = SPLIT
         for width in SCALAR_PARTS:
             nc.scalar.copy(out=out_grouped[:, at : at + width, last], in_=pages[last][:, at : at + width])

from contextlib import ExitStack

import concourse.mybir as mybir
from concourse.masks import make_identity

K, N, T, J = 512, 512, 2048, 1024
FLOPS = 3 * 2 * K * N * J

F32 = mybir.dt.float32
BF16 = mybir.dt.bfloat16
U32 = mybir.dt.uint32
I32 = mybir.dt.int32
U16 = mybir.dt.uint16
U8 = mybir.dt.uint8
E4M3 = mybir.dt.float8_e4m3fn_x4
E5M2 = mybir.dt.float8_e5m2_x4
ADD = mybir.AluOpType.add
SUB = mybir.AluOpType.subtract
MULT = mybir.AluOpType.mult

P = 128
PACK = 4
CHUNK = 256
HALF = 512
BACK = 128
RUN = 4
SPLIT = 768
WOVEN = 1536
VECTOR_PARTS = (384, 384)
SCALAR_PARTS = (384, 384, 384, 128)


def flat(tile):
    return tile[:].rearrange("p c i -> p (c i)")


def tile_list_embg_tgf32_resP_kernel(tc, dy, w, res, wgo, offs, out_0, out_1, out_2):
    nc = tc.nc
    chunks = J // CHUNK
    halves = J // HALF
    with ExitStack() as ctx:
        keep = ctx.enter_context(tc.tile_pool(name="keep", bufs=1))
        psum = ctx.enter_context(tc.psum_pool(name="psum", bufs=1))

        offsets = keep.tile([P, J // 16], U16, name="offsets")
        dy_rows = dy.rearrange("(p i) j -> p i j", i=PACK)
        w_rows = w.rearrange("(p i) n -> p i n", i=PACK)
        res_rows = res.rearrange("(p i) j -> p i j", i=PACK)
        out_rows = out_0.rearrange("(p i) t -> p i t", i=PACK)

        dy_raw = [keep.tile([P, PACK, CHUNK], F32, name="dy_raw%d" % c, tag="raw%d" % c, align_bytes=64) for c in range(chunks)]
        w_raw = [keep.tile([P, PACK, N // 2], F32, name="w_raw%d" % h, align_bytes=64) for h in range(2)]
        res_sb = [[keep.tile([P, HALF], F32, name="res%d_%d" % (i, h), tag="page3" if i * halves + h == 3 else "res%d" % (i * halves + h), align_bytes=64) for h in range(halves)] for i in range(PACK)]
        wgo_sb = [keep.tile([P, HALF], F32, name="wgo%d" % h) for h in range(halves)]

        def load_dy(c):
            nc.sync.dma_start(out=dy_raw[c][:], in_=dy_rows[:, :, c * CHUNK : (c + 1) * CHUNK])

        def load_res(i, h):
            nc.sync.dma_start(out=res_sb[i][h][:], in_=res_rows[:, i, h * HALF : (h + 1) * HALF])

        def load_wgo(h):
            nc.sync.dma_start(out=wgo_sb[h][:], in_=wgo[:, h * HALF : (h + 1) * HALF])

        for c in range(chunks):
            load_dy(c)
        for h in range(2):
            nc.sync.dma_start(out=w_raw[h][:], in_=w_rows[:, :, h * (N // 2) : (h + 1) * (N // 2)])
        load_res(0, 0)
        nc.sync.dma_start(offsets[:], offs)
        load_wgo(0)
        load_res(0, 1)
        load_wgo(1)
        for i in range(1, PACK):
            for h in range(halves):
                load_res(i, h)

        eye = keep.tile([P, P], BF16, name="eye")
        make_identity(nc, eye[:])
        eye_codes = keep.tile([P, K], U32, name="eye_codes", align_bytes=64)
        eye_scales = keep.tile([P, K], U8, name="eye_scales", align_bytes=64)
        eye_grouped = keep.tile([P, PACK * (K + 1)], BF16, name="eye_grouped", tag="first", align_bytes=64)
        nc.vector.memset(eye_grouped[:].bitcast(I32), 0)
        nc.vector.tensor_copy(out=eye_grouped[:].rearrange("p (i x) -> p i x", i=PACK)[:, :, 0:K:PACK],
                              in_=eye[:].unsqueeze(1).to_broadcast([P, PACK, P]))
        nc.vector.quantize_mx(out=eye_codes[:].bitcast(E4M3), scales=eye_scales[:], in_=eye_grouped[:, 0 : PACK * K])

        pages = [None] * PACK

        q_codes = [None] * chunks
        q_scales = [keep.tile([P, HALF], U8, name="q_scales%d" % h, align_bytes=64) for h in range(halves)]
        r_codes = [None] * halves
        r_scales = [keep.tile([P, HALF], U8, name="r_scales%d" % h, align_bytes=64) for h in range(halves)]
        w_scales = keep.tile([P, N], U8, name="w_scales", align_bytes=64)
        left = [keep.tile([P, HALF, PACK], BF16, name="left%d" % h, tag="page%d" % (1 + h), align_bytes=64)
                for h in range(halves)]
        sums = {}
        dx = {}

        def place(c):
            h, part = divmod(c, HALF // CHUNK)
            return h, part * CHUNK

        def round_dy(c, grouped):
            copy = nc.vector.tensor_copy if c == 0 else nc.scalar.copy
            copy(out=grouped.rearrange("p (c r) i -> p c i r", r=RUN),
                 in_=dy_raw[c][:].rearrange("p i (c r) -> p c i r", r=RUN))

        def first_tier(c, grouped, codes):
            h, at = place(c)
            q_codes[c] = codes
            nc.vector.quantize_mx(out=codes.bitcast(E5M2), scales=q_scales[h][:, at : at + CHUNK],
                                  in_=grouped.rearrange("p c i -> p (c i)"))

        def leftover(c):
            h, at = place(c)
            for b in range(CHUNK // BACK):
                cols = slice(at + b * BACK, at + (b + 1) * BACK)
                local = slice(b * BACK, (b + 1) * BACK)
                back = psum.tile([P, PACK, BACK], F32, name="back", bufs=4)
                for i in range(PACK):
                    nc.tensor.matmul_mx(
                        out=back[:, i, :],
                        lhsT=eye_codes[:, i * P : (i + 1) * P].bitcast(E4M3),
                        lhsT_scale=eye_scales[:, i * P : (i + 1) * P],
                        rhs=q_codes[c][:, local].bitcast(E5M2), rhs_scale=q_scales[h][:, cols],
                        start=True, stop=True)
                nc.vector.tensor_tensor(
                    out=left[h][:, cols, :].rearrange("p (c r) i -> p c i r", r=2),
                    in0=dy_raw[c][:, :, local].rearrange("p i (c r) -> p c i r", r=2),
                    in1=back[:].rearrange("p i (c r) -> p c i r", r=2), op=SUB)

        def second_tier(h):
            r_codes[h] = keep.tile([P, HALF], U32, name="r_codes%d" % h, tag=("grouped", "w_grouped")[h], align_bytes=64)
            nc.vector.quantize_mx(out=r_codes[h][:].bitcast(E4M3), scales=r_scales[h][:], in_=flat(left[h]))

        def quantize_w():
            grouped = keep.tile([P, PACK, P, PACK], BF16, name="w_grouped", tag="w_grouped", align_bytes=64)
            for h in range(2):
                nc.scalar.copy(
                    out=grouped[:, :, h * (P // 2) : (h + 1) * (P // 2), :].rearrange("p i m b -> p m b i"),
                    in_=w_raw[h][:].rearrange("p b (m i) -> p m b i", i=PACK))
            codes = keep.tile([P, N], U32, name="w_codes", tag="raw3", align_bytes=64)
            nc.vector.quantize_mx(out=codes[:].bitcast(E4M3), scales=w_scales[:],
                                  in_=grouped[:].rearrange("p i m b -> p (i m b)"))
            return codes

        def product(i, h):
            acc = psum.tile([P, HALF], F32, name="acc", bufs=4)
            cols = slice(i * P, (i + 1) * P)
            weights = w_codes[:, cols].bitcast(E4M3)
            nc.tensor.matmul_mx(out=acc[:], lhsT=weights, lhsT_scale=w_scales[:, cols],
                                rhs=r_codes[h][:].bitcast(E4M3), rhs_scale=r_scales[h][:], start=True, stop=False)
            for part in range(HALF // CHUNK):
                local = slice(part * CHUNK, (part + 1) * CHUNK)
                nc.tensor.matmul_mx(out=acc[:, local], lhsT=weights, lhsT_scale=w_scales[:, cols],
                                    rhs=q_codes[h * (HALF // CHUNK) + part].bitcast(E5M2),
                                    rhs_scale=q_scales[h][:, local], start=False, stop=(part == HALF // CHUNK - 1))
            if i + h == 0:
                dx[i, h] = acc
            else:
                dx[i, h] = keep.tile([P, HALF], F32, name="dx%d_%d" % (i, h))
                nc.scalar.copy(out=dx[i, h][:], in_=acc[:])

        def weigh(i, h):
            step = i * halves + h
            engine = nc.gpsimd if step else nc.vector
            tag = {0: "total0", 1: "total1", 4: "page3"}.get(step, "res%d" % (step - 1))
            total = keep.tile([P, HALF], F32, name="total%d" % step, tag=tag, align_bytes=64)
            engine.tensor_tensor(out=total[:], in0=dx[i, h][:], in1=res_sb[i][h][:], op=ADD)
            sums[i, h] = keep.tile([P, HALF], F32, name="weighted%d" % step)
            engine.tensor_tensor(out=sums[i, h][:], in0=total[:], in1=wgo_sb[h][:], op=MULT)

        def clear_page(i):
            pages[i] = keep.tile([P, T], F32, name="page%d" % i, tag="page%d" % i, align_bytes=64)
            nc.gpsimd.memset(pages[i][:], 0.0)

        def scatter(i, h):
            listed = offsets[:, h * (HALF // 16) : (h + 1) * (HALF // 16)]
            nc.vector.tensor_copy(out=pages[i][:].indirect(listed), in_=sums[i, h][:])

        out_grouped = keep.tile([P, T, PACK], BF16, name="out_grouped", align_bytes=64)

        def store_page(i):
            nc.sync.dma_start(out=out_rows[:, i, :], in_=pages[i][:])

        grouped0 = keep.tile([P, CHUNK, PACK], BF16, name="dy_grouped0", tag="first", align_bytes=64)
        round_dy(0, grouped0[:])
        first_tier(0, grouped0[:], keep.tile([P, CHUNK], U32, name="q_codes0", align_bytes=64)[:])
        grouped1 = keep.tile([P, CHUNK, PACK], BF16, name="dy_grouped1", tag="page0", align_bytes=64)
        round_dy(1, grouped1[:])
        first_tier(1, grouped1[:], keep.tile([P, CHUNK], U32, name="q_codes1", tag="first", align_bytes=64)[:])
        clear_page(0)
        leftover(0)
        leftover(1)
        grouped23 = keep.tile([P, HALF, PACK], BF16, name="dy_grouped23", tag="grouped", align_bytes=64)
        codes23 = keep.tile([P, HALF], U32, name="q_codes23", tag="raw1", align_bytes=64)
        for part in range(2):
            local = slice(part * CHUNK, (part + 1) * CHUNK)
            round_dy(2 + part, grouped23[:, local, :])
            first_tier(2 + part, grouped23[:, local, :], codes23[:, local])
        second_tier(0)
        clear_page(1)
        leftover(2)
        leftover(3)
        w_codes = quantize_w()
        second_tier(1)
        for i in range(PACK):
            for h in range(halves):
                product(i, h)
        clear_page(2)
        weigh(0, 0)
        last = PACK - 1
        staged = keep.tile([P, 2, SPLIT], BF16, name="staged", align_bytes=64)
        waiting = keep.tile([P, last, T - WOVEN], BF16, name="waiting", align_bytes=64)

        def weave(copy, cols, planes, rounded):
            copy(out=out_grouped[:, cols, planes].rearrange("p (c r) i -> p c i r", r=2),
                 in_=rounded[:].rearrange("p i (c r) -> p c i r", r=2))

        for i in range(PACK):
            scatter(i, 0)
            weigh(i, 1)
            scatter(i, 1)
            if i < last:
                weigh(i + 1, 0)
            if i == 1:
                clear_page(last)
            store_page(i)
            if i < last:
                first = 0 if i < last - 1 else SPLIT
                if first:
                    nc.scalar.copy(out=staged[:, 0, :], in_=pages[i][:, :SPLIT])
                nc.scalar.copy(out=waiting[:, i, :], in_=pages[i][:, WOVEN:])
                nc.scalar.copy(out=out_grouped[:, first:WOVEN, i], in_=pages[i][:, first:WOVEN])
                if first:
                    weave(nc.scalar.copy, slice(WOVEN, T), slice(0, last), waiting)

        y_codes = keep.tile([P, T], U32, name="y_codes", align_bytes=64)
        y_scales = keep.tile([P, T], U8, name="y_scales", align_bytes=64)
        words = out_1[0].rearrange("p t i -> p (t i)").bitcast(I32)
        nc.vector.tensor_copy(out=staged[:, 1, :], in_=pages[last][:, :SPLIT])
        weave(nc.vector.tensor_copy, slice(0, SPLIT), slice(last - 1, PACK), staged)
        at = SPLIT
        for width in SCALAR_PARTS:
            nc.scalar.copy(out=out_grouped[:, at : at + width, last], in_=pages[last][:, at : at + width])
            at = at + width
        at = 0
        for width in VECTOR_PARTS + SCALAR_PARTS:
            cols = slice(at, at + width)
            nc.vector.quantize_mx(out=y_codes[:, cols].bitcast(E4M3), scales=y_scales[:, cols],
                                  in_=out_grouped[:, cols, :].rearrange("p t i -> p (t i)"))
            nc.sync.dma_start(out=words[:, cols], in_=y_codes[:, cols].bitcast(I32))
            at = at + width
        for q in range(4):
            queue = nc.sync if q % 2 == 0 else nc.scalar
            queue.dma_start(out=out_2[0, 4 * q : 4 * q + 4, :].bitcast(I32),
                            in_=y_scales[32 * q : 32 * q + 4, :].bitcast(I32))
